import numpy as np
import ml_dtypes


def mxq(x, axis, fmt="e4m3"):
    dtype, down = {"e4m3": (ml_dtypes.float8_e4m3fn, 7), "e5m2": (ml_dtypes.float8_e5m2, 14)}[fmt]
    v = np.moveaxis(np.asarray(x, np.float32).astype(ml_dtypes.bfloat16).astype(np.float64), axis, -1)
    blocks = v.reshape(v.shape[:-1] + (-1, 32))
    amax = np.abs(blocks).max(-1, keepdims=True)
    byte = np.maximum(np.where(amax > 0, np.frexp(amax)[1] - 1 + 127, 0) - down, 1)
    scale = np.exp2(byte - 127.0)
    codes = (blocks / scale).astype(np.float32).astype(dtype).astype(np.float64)
    return np.moveaxis((codes * scale).reshape(v.shape), -1, axis)


WIDE = False


def mx_kscale(k):
    if not WIDE:
        return np.ones(k)
    levels = np.array([10, -10, 5, -5, 0])
    if k % 512:
        return np.exp2(np.random.permutation(np.resize(levels, k // 32))).repeat(32)
    a = np.empty((k // 512, 16))
    for p in range(k // 512):
        a[p, :8] = np.random.permutation(np.resize(levels, 8))
        for g in range(8):
            far = levels[np.abs(levels - a[p, g]) >= 10]
            a[p, g + 8] = far[np.random.randint(len(far))]
    return np.exp2(a.ravel()).repeat(32)


def f64(x):
    return np.asarray(x).astype(np.float64)


def striped(idx):
    return np.tile(np.asarray(idx).reshape(-1, 16).T, (8, 1)).astype(np.uint16)


def unstriped(offs):
    return offs[:16].T.reshape(-1).astype(np.int64)


E2M1 = np.array([0.0, 0.5, 1.0, 1.5, 2.0, 3.0, 4.0, 6.0, -0.0, -0.5, -1.0, -1.5, -2.0, -3.0, -4.0, -6.0])


def pack_weight(w, fmt):
    k, n = w.shape
    w = f64(np.asarray(w, np.float32).astype(ml_dtypes.bfloat16)).reshape(k // 32, 32, n)
    amax = np.abs(w).max(1)
    if fmt == "e4m3":
        byte = np.frexp(amax)[1] - 1 + 127 - 7
    else:
        mant, ex = np.frexp(amax / 6.0)
        byte = np.where(mant > 0.5, ex, ex - 1) + 127
    byte = np.clip(np.where(amax > 0, byte, 1), 1, 254)
    scaled = (w * np.exp2(127.0 - byte)[:, None, :]).reshape(k, n).astype(np.float32)
    by_word = np.ascontiguousarray(scaled.reshape(k // 512, 128, 4, n).transpose(0, 1, 3, 2))
    if fmt == "e4m3":
        words = by_word.astype(ml_dtypes.float8_e4m3fn).view(np.uint8)
    else:
        c = by_word.astype(ml_dtypes.float4_e2m1fn).view(np.uint8) & 0xF
        words = (c[..., 0::2] | (c[..., 1::2] << 4)).reshape(k // 512, 128, 2 * n)
    return np.ascontiguousarray(words), np.ascontiguousarray(byte.astype(np.uint8).reshape(k // 512, 16, n))


def unpack_weight(words, scales, fmt):
    g, _, n = scales.shape
    words = np.ascontiguousarray(words).reshape(g, 128, n, -1)
    if fmt == "e4m3":
        vals = words.view(ml_dtypes.float8_e4m3fn).astype(np.float64)
    else:
        nib = np.empty((g, 128, n, 4), np.uint8)
        nib[..., 0::2] = words & 0xF
        nib[..., 1::2] = words >> 4
        vals = E2M1[nib]
    vals = vals * np.repeat(np.exp2(scales.astype(np.float64) - 127.0), 8, axis=1)[..., None]
    return vals.transpose(0, 1, 3, 2).reshape(g * 512, n)


D, K, T, U, I, J, C = 512, 512, 2048, 1024, 512, 512, 256


def setup_inputs():
    n = np.random.standard_normal
    idx = np.random.permutation(T)[:I]
    idx2 = np.random.permutation(U)[:J]
    idx3 = np.random.permutation(J)[:C]
    fd = mx_kscale(D)
    fk = mx_kscale(K)
    pagesp = pack_weight(n((D, T)) / fd[:, None], "e4m3")
    wap = pack_weight(n((D, K)) * 1.0 / np.sqrt(D) * fd[:, None] * fk, "e2m1")
    notesp = pack_weight(n((D, U)) / fd[:, None], "e2m1")
    wbp = pack_weight(n((D, K)) * 1.0 / np.sqrt(D) * fd[:, None], "e4m3")
    return {
        "pages_words": pagesp[0],
        "pages_scales": pagesp[1],
        "wa_words": wap[0],
        "wa_scales": wap[1],
        "notes_words": notesp[0],
        "notes_scales": notesp[1],
        "wb_words": wbp[0],
        "wb_scales": wbp[1],
        "kf": (np.random.uniform(0.03, 0.09, (K, 1)) / fk[:, None]).astype(np.float32),
        "offs": striped(idx),
        "offs2": striped(idx2),
        "offs3": striped(idx3),
    }


def reference(pages_words, pages_scales, wa_words, wa_scales, notes_words, notes_scales, wb_words, wb_scales, kf, offs, offs2, offs3):
    idx = unstriped(offs)
    idx2 = unstriped(offs2)
    idx3 = unstriped(offs3)
    pagesu = unpack_weight(pages_words, pages_scales, "e4m3")
    wau = unpack_weight(wa_words, wa_scales, "e2m1")
    notesu = unpack_weight(notes_words, notes_scales, "e2m1")
    wbu = unpack_weight(wb_words, wb_scales, "e4m3")
    pagesidxg = pagesu[:, idx]
    z = wau.T @ pagesidxg
    notesidx2g = notesu[:, idx2]
    h2 = wbu.T @ notesidx2g
    h3 = h2 * f64(kf)
    zq = mxq(z, 0, "e4m3")
    h3q = mxq(h3, 0, "e4m3")
    s = zq.T @ h3q
    ts = np.max(s, axis=1, keepdims=True)
    y = np.exp(s[:, idx3] - ts)
    return y

@@ -1,0 +1,188 @@
+from contextlib import ExitStack
+
+import concourse.mybir as mybir
+from concourse.masks import make_identity
+
+F32 = mybir.dt.float32
+BF16 = mybir.dt.bfloat16
+I32 = mybir.dt.int32
+U32 = mybir.dt.uint32
+U16 = mybir.dt.uint16
+U8 = mybir.dt.uint8
+E4M3 = mybir.dt.float8_e4m3fn_x4
+E2M1 = mybir.dt.float4_e2m1fn_x4
+ACT = mybir.ActivationFunctionType
+ALU = mybir.AluOpType
+
+P = 128
+PACK = 4
+D, K, T, U, I, J, C = 512, 512, 2048, 1024, 512, 512, 256
+HALF = 256
+FLOPS = 2 * (D * K * I + D * K * J + K * I * J)
+
+
+def load_scale_rows(queue, plane, rows):
+    for r in range(4):
+        queue.dma_start(out=plane[r:P:32, :].bitcast(I32), in_=rows[0, r:16:4, :].bitcast(I32))
+
+
+def deal(nc, dst, src, run):
+    nc.vector.tensor_copy(
+        out=dst.rearrange("p (t q r) -> p t q r", t=PACK, r=run),
+        in_=src.rearrange("p (q t r) -> p t q r", t=PACK, r=run),
+    )
+
+
+def tile_attend_matchtable_kernel(
+    tc, pages_words, pages_scales, wa_words, wa_scales, notes_words, notes_scales,
+    wb_words, wb_scales, kf, offs, offs2, offs3, out,
+):
+    nc = tc.nc
+    with ExitStack() as ctx:
+        lists = ctx.enter_context(tc.tile_pool(name="lists", bufs=1))
+        sb = ctx.enter_context(tc.tile_pool(name="sb", bufs=1))
+        psum = ctx.enter_context(tc.psum_pool(name="psum", bufs=1))
+
+        def tile(shape, dtype, name):
+            return sb.tile(shape, dtype, name=name, align_bytes=64)
+
+        def bank(n, shape, name):
+            return psum.tile(shape, F32, name=name, tag="bank%d" % n)
+
+        page_list = lists.tile([P, I // 16], U16, name="page_list")
+        note_list = lists.tile([P, J // 16], U16, name="note_list")
+        column_list = lists.tile([P, C // 16], U16, name="column_list")
+
+        pages_w = tile([P, T], U32, "pages_w")
+        pages_s = tile([P, T], U8, "pages_s")
+        notes_w = tile([P, U], U16, "notes_w")
+        notes_s = tile([P, U], U8, "notes_s")
+        wa_w_raw = tile([P, K], U16, "wa_w_raw")
+        wa_s_raw = tile([P, K], U8, "wa_s_raw")
+        wb_w_raw = tile([P, K], U32, "wb_w_raw")
+        wb_s_raw = tile([P, K], U8, "wb_s_raw")
+        kf_rows = tile([P, P], F32, "kf_rows")
+        identity = tile([P, P], F32, "identity")
+
+        nc.vector.memset(notes_s[:].bitcast(I32), 0)
+        nc.vector.memset(wb_s_raw[:].bitcast(I32), 0)
+        nc.vector.memset(pages_s[:].bitcast(I32), 0)
+        nc.gpsimd.memset(kf_rows[:], 0.0)
+        make_identity(nc, identity[:])
+        nc.vector.memset(wa_s_raw[:].bitcast(I32), 0)
+
+        nc.sync.dma_start(note_list[:], offs2)
+        nc.sync.dma_start(out=notes_w[:].bitcast(I32), in_=notes_words[0].bitcast(I32))
+        load_scale_rows(nc.scalar, notes_s, notes_scales)
+        nc.sync.dma_start(
+            out=wb_w_raw[:].bitcast(I32), in_=wb_words[0].rearrange("p n t -> p (n t)").bitcast(I32))
+        nc.sync.dma_start(
+            out=pages_w[:].bitcast(I32), in_=pages_words[0].rearrange("p n t -> p (n t)").bitcast(I32))
+        load_scale_rows(nc.scalar, wb_s_raw, wb_scales)
+        nc.scalar.dma_start(
+            out=kf_rows[0:PACK, :], in_=kf.rearrange("(q t r) o -> t q (r o)", t=PACK, r=8))
+        nc.sync.dma_start(page_list[:], offs)
+        nc.sync.dma_start(out=wa_w_raw[:].bitcast(I32), in_=wa_words[0].bitcast(I32))
+        nc.sync.dma_start(column_list[:], offs3)
+        load_scale_rows(nc.sync, pages_s, pages_scales)
+        load_scale_rows(nc.gpsimd, wa_s_raw, wa_scales)
+
+        kf_turned = bank(7, [P, P], "kf_turned")
+        nc.tensor.transpose(kf_turned[:], kf_rows[:], identity[:])
+        kf_cols = tile([P, PACK], F32, "kf_cols")
+        nc.scalar.copy(out=kf_cols[:], in_=kf_turned[:, 0:PACK])
+
+        wb_w = tile([P, K], U32, "wb_w")
+        wb_s = tile([P, K], U8, "wb_s")
+        h_planes = []
+        for half in range(2):
+            cols = slice(half * HALF // 16, (half + 1) * HALF // 16)
+            nw = tile([P, HALF], U16, "note_w%d" % half)
+            ns = tile([P, HALF], U8, "note_s%d" % half)
+            nc.vector.tensor_copy(nw[:], notes_w[:].indirect(note_list[:, cols]))
+            nc.vector.tensor_copy(ns[:], notes_s[:].indirect(note_list[:, cols]))
+            if half == 0:
+                deal(nc, wb_w[:], wb_w_raw[:], 8)
+                deal(nc, wb_s[:].bitcast(I32), wb_s_raw[:].bitcast(I32), 2)
+            planes = tile([P, PACK, HALF], BF16, "h_planes%d" % half)
+            for pair in range(2):
+                acc = bank(2 * half + pair, [P, 2, HALF], "h_acc")
+                for e in range(2):
+                    t = 2 * pair + e
+                    nc.tensor.matmul_mx(
+                        out=acc[:, e, :],
+                        lhsT=wb_w[:, t * P:(t + 1) * P].bitcast(E4M3), lhsT_scale=wb_s[:, t * P:(t + 1) * P],
+                        rhs=nw[:].bitcast(E2M1), rhs_scale=ns[:], start=True, stop=True)
+                for e in range(2):
+                    t = 2 * pair + e
+                    nc.scalar.activation(
+                        out=planes[:, t, :], in_=acc[:, e, :], func=ACT.Copy, scale=kf_cols[:, t:t + 1])
+            h_planes.append(planes)
+
+        wa_w = tile([P, K], U16, "wa_w")
+        wa_s = tile([P, K], U8, "wa_s")
+        z_grouped = []
+        for half in range(2):
+            cols = slice(half * HALF // 16, (half + 1) * HALF // 16)
+            pw = tile([P, HALF], U32, "page_w%d" % half)
+            ps = tile([P, HALF], U8, "page_s%d" % half)
+            nc.vector.tensor_copy(pw[:], pages_w[:].indirect(page_list[:, cols]))
+            nc.vector.tensor_copy(ps[:], pages_s[:].indirect(page_list[:, cols]))
+            if half == 0:
+                deal(nc, wa_w[:], wa_w_raw[:], 8)
+                deal(nc, wa_s[:].bitcast(I32), wa_s_raw[:].bitcast(I32), 2)
+            for e in range(2):
+                chunk = 2 * half + e
+                acc = bank(4 + chunk, [P, PACK, P], "z_acc")
+                for t in range(PACK):
+                    nc.tensor.matmul_mx(
+                        out=acc[:, t, :],
+                        lhsT=wa_w[:, t * P:(t + 1) * P].bitcast(E2M1), lhsT_scale=wa_s[:, t * P:(t + 1) * P],
+                        rhs=pw[:, e * P:(e + 1) * P].bitcast(E4M3), rhs_scale=ps[:, e * P:(e + 1) * P],
+                        start=True, stop=True)
+                grouped = tile([P, P, PACK], BF16, "z_grouped%d" % chunk)
+                nc.scalar.copy(out=grouped[:], in_=acc[:].rearrange("p t i -> p i t"))
+                z_grouped.append(grouped)
+
+        h_codes = tile([P, J], U32, "h_codes")
+        h_scales = tile([P, J], U8, "h_scales")
+        h_grouped = []
+        for half in range(2):
+            grouped = tile([P, HALF, PACK], BF16, "h_grouped%d" % half)
+            nc.vector.tensor_copy(
+                out=grouped[:].rearrange("p (c i) t -> p c t i", i=4),
+                in_=h_planes[half][:].rearrange("p t (c i) -> p c t i", i=4))
+            h_grouped.append(grouped)
+        for half in range(2):
+            cols = slice(half * HALF, (half + 1) * HALF)
+            nc.vector.quantize_mx(
+                out=h_codes[:, cols].bitcast(E4M3), scales=h_scales[:, cols],
+                in_=h_grouped[half][:].rearrange("p j t -> p (j t)"))
+
+        z_codes = []
+        for chunk in range(4):
+            codes = tile([P, P], U32, "z_codes%d" % chunk)
+            scales = tile([P, P], U8, "z_scales%d" % chunk)
+            nc.vector.quantize_mx(
+                out=codes[:].bitcast(E4M3), scales=scales[:],
+                in_=z_grouped[chunk][:].rearrange("p i t -> p (i t)"))
+            z_codes.append((codes, scales))
+
+        for chunk in range(4):
+            codes, scales = z_codes[chunk]
+            acc = bank(chunk, [P, J], "s_acc")
+            nc.tensor.matmul_mx(
+                out=acc[:], lhsT=codes[:].bitcast(E4M3), lhsT_scale=scales[:],
+                rhs=h_codes[:].bitcast(E4M3), rhs_scale=h_scales[:], start=True, stop=True)
+            table = tile([P, J], F32, "table%d" % chunk)
+            top = tile([P, 1], F32, "top%d" % chunk)
+            nc.vector.tensor_scalar(
+                out=table[:], in0=acc[:], scalar1=1.0, scalar2=None, op0=ALU.mult, op1=ALU.max,
+                accum_out=top[:])
+            minus_top = tile([P, 1], F32, "minus_top%d" % chunk)
+            nc.gpsimd.tensor_scalar(
+                out=minus_top[:], in0=top[:], scalar1=-1.0, scalar2=0.0, op0=ALU.mult, op1=ALU.add)
+            result = tile([P, C], F32, "result%d" % chunk)
+            nc.scalar.activation(
+                out=result[:], in_=table[:].indirect(column_list[:]), func=ACT.Exp, bias=minus_top[:])
+            nc.sync.dma_start(out=out[chunk * P:(chunk + 1) * P, :], in_=result[:])

@@ -22,8 +22,10 @@ FLOPS = 2 * (D * K * I + D * K * J + K * I * J)
 
 
 def load_scale_rows(queue, plane, rows):
-    for r in range(4):
-        queue.dma_start(out=plane[r:P:32, :].bitcast(I32), in_=rows[0, r:16:4, :].bitcast(I32))
+    for quadrant in range(4):
+        queue.dma_start(
+            out=plane[32 * quadrant:32 * quadrant + 4, :].bitcast(I32),
+            in_=rows[0, 4 * quadrant:4 * quadrant + 4, :].bitcast(I32))
 
 
 def deal(nc, dst, src, run):
@@ -65,45 +67,45 @@ def tile_attend_matchtable_kernel(
         identity = tile([P, P], F32, "identity")
 
         nc.vector.memset(notes_s[:].bitcast(I32), 0)
-        nc.vector.memset(wb_s_raw[:].bitcast(I32), 0)
+        nc.vector.memset(kf_rows[:], 0.0)
         nc.vector.memset(pages_s[:].bitcast(I32), 0)
-        nc.gpsimd.memset(kf_rows[:], 0.0)
-        make_identity(nc, identity[:])
         nc.vector.memset(wa_s_raw[:].bitcast(I32), 0)
+        nc.gpsimd.memset(wb_s_raw[:].bitcast(I32), 0)
+        load_scale_rows(nc.gpsimd, wb_s_raw, wb_scales)
+        make_identity(nc, identity[:])
 
-        nc.sync.dma_start(note_list[:], offs2)
         nc.sync.dma_start(out=notes_w[:].bitcast(I32), in_=notes_words[0].bitcast(I32))
-        load_scale_rows(nc.scalar, notes_s, notes_scales)
+        nc.sync.dma_start(note_list[:], offs2)
+        load_scale_rows(nc.sync, notes_s, notes_scales)
         nc.sync.dma_start(
             out=wb_w_raw[:].bitcast(I32), in_=wb_words[0].rearrange("p n t -> p (n t)").bitcast(I32))
         nc.sync.dma_start(
             out=pages_w[:].bitcast(I32), in_=pages_words[0].rearrange("p n t -> p (n t)").bitcast(I32))
-        load_scale_rows(nc.scalar, wb_s_raw, wb_scales)
-        nc.scalar.dma_start(
+        nc.sync.dma_start(
             out=kf_rows[0:PACK, :], in_=kf.rearrange("(q t r) o -> t q (r o)", t=PACK, r=8))
         nc.sync.dma_start(page_list[:], offs)
-        nc.sync.dma_start(out=wa_w_raw[:].bitcast(I32), in_=wa_words[0].bitcast(I32))
-        nc.sync.dma_start(column_list[:], offs3)
         load_scale_rows(nc.sync, pages_s, pages_scales)
-        load_scale_rows(nc.gpsimd, wa_s_raw, wa_scales)
+        nc.sync.dma_start(out=wa_w_raw[:].bitcast(I32), in_=wa_words[0].bitcast(I32))
+        load_scale_rows(nc.sync, wa_s_raw, wa_scales)
+        nc.sync.dma_start(column_list[:], offs3)
 
         kf_turned = bank(7, [P, P], "kf_turned")
         nc.tensor.transpose(kf_turned[:], kf_rows[:], identity[:])
         kf_cols = tile([P, PACK], F32, "kf_cols")
         nc.scalar.copy(out=kf_cols[:], in_=kf_turned[:, 0:PACK])
 
+        note_w = tile([P, J], U16, "note_w")
+        note_s = tile([P, J], U8, "note_s")
+        nc.vector.tensor_copy(note_w[:], notes_w[:].indirect(note_list[:]))
+        nc.vector.tensor_copy(note_s[:], notes_s[:].indirect(note_list[:]))
+
         wb_w = tile([P, K], U32, "wb_w")
         wb_s = tile([P, K], U8, "wb_s")
+        deal(nc, wb_w[:], wb_w_raw[:], 8)
+        deal(nc, wb_s[:].bitcast(I32), wb_s_raw[:].bitcast(I32), 2)
         h_planes = []
         for half in range(2):
-            cols = slice(half * HALF // 16, (half + 1) * HALF // 16)
-            nw = tile([P, HALF], U16, "note_w%d" % half)
-            ns = tile([P, HALF], U8, "note_s%d" % half)
-            nc.vector.tensor_copy(nw[:], notes_w[:].indirect(note_list[:, cols]))
-            nc.vector.tensor_copy(ns[:], notes_s[:].indirect(note_list[:, cols]))
-            if half == 0:
-                deal(nc, wb_w[:], wb_w_raw[:], 8)
-                deal(nc, wb_s[:].bitcast(I32), wb_s_raw[:].bitcast(I32), 2)
+            cols = slice(half * HALF, (half + 1) * HALF)
             planes = tile([P, PACK, HALF], BF16, "h_planes%d" % half)
             for pair in range(2):
                 acc = bank(2 * half + pair, [P, 2, HALF], "h_acc")
@@ -112,37 +114,34 @@ def tile_attend_matchtable_kernel(
                     nc.tensor.matmul_mx(
                         out=acc[:, e, :],
                         lhsT=wb_w[:, t * P:(t + 1) * P].bitcast(E4M3), lhsT_scale=wb_s[:, t * P:(t + 1) * P],
-                        rhs=nw[:].bitcast(E2M1), rhs_scale=ns[:], start=True, stop=True)
+                        rhs=note_w[:, cols].bitcast(E2M1), rhs_scale=note_s[:, cols], start=True, stop=True)
                 for e in range(2):
                     t = 2 * pair + e
                     nc.scalar.activation(
                         out=planes[:, t, :], in_=acc[:, e, :], func=ACT.Copy, scale=kf_cols[:, t:t + 1])
             h_planes.append(planes)
 
+        page_w = tile([P, I], U32, "page_w")
+        nc.vector.tensor_copy(page_w[:], pages_w[:].indirect(page_list[:]))
+        page_s = tile([P, I], U8, "page_s")
+        nc.vector.tensor_copy(page_s[:], pages_s[:].indirect(page_list[:]))
         wa_w = tile([P, K], U16, "wa_w")
         wa_s = tile([P, K], U8, "wa_s")
+        deal(nc, wa_w[:], wa_w_raw[:], 8)
+        deal(nc, wa_s[:].bitcast(I32), wa_s_raw[:].bitcast(I32), 2)
         z_grouped = []
-        for half in range(2):
-            cols = slice(half * HALF // 16, (half + 1) * HALF // 16)
-            pw = tile([P, HALF], U32, "page_w%d" % half)
-            ps = tile([P, HALF], U8, "page_s%d" % half)
-            nc.vector.tensor_copy(pw[:], pages_w[:].indirect(page_list[:, cols]))
-            nc.vector.tensor_copy(ps[:], pages_s[:].indirect(page_list[:, cols]))
-            if half == 0:
-                deal(nc, wa_w[:], wa_w_raw[:], 8)
-                deal(nc, wa_s[:].bitcast(I32), wa_s_raw[:].bitcast(I32), 2)
-            for e in range(2):
-                chunk = 2 * half + e
-                acc = bank(4 + chunk, [P, PACK, P], "z_acc")
-                for t in range(PACK):
-                    nc.tensor.matmul_mx(
-                        out=acc[:, t, :],
-                        lhsT=wa_w[:, t * P:(t + 1) * P].bitcast(E2M1), lhsT_scale=wa_s[:, t * P:(t + 1) * P],
-                        rhs=pw[:, e * P:(e + 1) * P].bitcast(E4M3), rhs_scale=ps[:, e * P:(e + 1) * P],
-                        start=True, stop=True)
-                grouped = tile([P, P, PACK], BF16, "z_grouped%d" % chunk)
-                nc.scalar.copy(out=grouped[:], in_=acc[:].rearrange("p t i -> p i t"))
-                z_grouped.append(grouped)
+        for chunk in range(4):
+            cols = slice(chunk * P, (chunk + 1) * P)
+            acc = bank(4 + chunk, [P, PACK, P], "z_acc")
+            for t in range(PACK):
+                nc.tensor.matmul_mx(
+                    out=acc[:, t, :],
+                    lhsT=wa_w[:, t * P:(t + 1) * P].bitcast(E2M1), lhsT_scale=wa_s[:, t * P:(t + 1) * P],
+                    rhs=page_w[:, cols].bitcast(E4M3), rhs_scale=page_s[:, cols],
+                    start=True, stop=True)
+            grouped = tile([P, P, PACK], BF16, "z_grouped%d" % chunk)
+            nc.scalar.copy(out=grouped[:], in_=acc[:].rearrange("p t i -> p i t"))
+            z_grouped.append(grouped)
 
         h_codes = tile([P, J], U32, "h_codes")
         h_scales = tile([P, J], U8, "h_scales")

@@ -21,11 +21,19 @@ HALF = 256
 FLOPS = 2 * (D * K * I + D * K * J + K * I * J)
 
 
-def load_scale_rows(queue, plane, rows):
-    for quadrant in range(4):
+def load_scale_rows(queue, plane, rows, quadrants=range(4)):
+    for quadrant in quadrants:
         queue.dma_start(
             out=plane[32 * quadrant:32 * quadrant + 4, :].bitcast(I32),
             in_=rows[0, 4 * quadrant:4 * quadrant + 4, :].bitcast(I32))
+
+
+def fill_scale_rows(queue, plane, rows, quadrants=range(4)):
+    for quadrant in quadrants:
+        four = rows[0, 4 * quadrant:4 * quadrant + 4, :].bitcast(I32)
+        queue.dma_start(
+            out=plane[32 * quadrant:32 * quadrant + 32, :].bitcast(I32),
+            in_=four.unsqueeze(0).broadcast_to([8, 4, four.shape[1]]))
 
 
 def deal(nc, dst, src, run):
@@ -45,8 +53,8 @@ def tile_attend_matchtable_kernel(
         sb = ctx.enter_context(tc.tile_pool(name="sb", bufs=1))
         psum = ctx.enter_context(tc.psum_pool(name="psum", bufs=1))
 
-        def tile(shape, dtype, name):
-            return sb.tile(shape, dtype, name=name, align_bytes=64)
+        def tile(shape, dtype, name, tag=None):
+            return sb.tile(shape, dtype, name=name, tag=tag or name, align_bytes=64)
 
         def bank(n, shape, name):
             return psum.tile(shape, F32, name=name, tag="bank%d" % n)
@@ -56,35 +64,34 @@ def tile_attend_matchtable_kernel(
         column_list = lists.tile([P, C // 16], U16, name="column_list")
 
         pages_w = tile([P, T], U32, "pages_w")
-        pages_s = tile([P, T], U8, "pages_s")
+        pages_s = tile([P, T], U8, "pages_s", "staging2")
         notes_w = tile([P, U], U16, "notes_w")
         notes_s = tile([P, U], U8, "notes_s")
         wa_w_raw = tile([P, K], U16, "wa_w_raw")
-        wa_s_raw = tile([P, K], U8, "wa_s_raw")
+        wa_s_raw = tile([P, K], U8, "wa_s_raw", "staging0")
         wb_w_raw = tile([P, K], U32, "wb_w_raw")
         wb_s_raw = tile([P, K], U8, "wb_s_raw")
         kf_rows = tile([P, P], F32, "kf_rows")
         identity = tile([P, P], F32, "identity")
 
-        nc.vector.memset(notes_s[:].bitcast(I32), 0)
-        nc.vector.memset(kf_rows[:], 0.0)
-        nc.vector.memset(pages_s[:].bitcast(I32), 0)
+        nc.vector.memset(pages_s[0:64, :].bitcast(I32), 0)
         nc.vector.memset(wa_s_raw[:].bitcast(I32), 0)
-        nc.gpsimd.memset(wb_s_raw[:].bitcast(I32), 0)
-        load_scale_rows(nc.gpsimd, wb_s_raw, wb_scales)
+        nc.gpsimd.memset(kf_rows[:], 0.0)
+        nc.gpsimd.dma_start(
+            out=kf_rows[0:PACK, :], in_=kf.rearrange("(q t r) o -> t q (r o)", t=PACK, r=8))
         make_identity(nc, identity[:])
+        load_scale_rows(nc.gpsimd, pages_s, pages_scales, range(0, 2))
 
         nc.sync.dma_start(out=notes_w[:].bitcast(I32), in_=notes_words[0].bitcast(I32))
         nc.sync.dma_start(note_list[:], offs2)
-        load_scale_rows(nc.sync, notes_s, notes_scales)
+        fill_scale_rows(nc.sync, notes_s, notes_scales)
         nc.sync.dma_start(
             out=wb_w_raw[:].bitcast(I32), in_=wb_words[0].rearrange("p n t -> p (n t)").bitcast(I32))
         nc.sync.dma_start(
             out=pages_w[:].bitcast(I32), in_=pages_words[0].rearrange("p n t -> p (n t)").bitcast(I32))
-        nc.sync.dma_start(
-            out=kf_rows[0:PACK, :], in_=kf.rearrange("(q t r) o -> t q (r o)", t=PACK, r=8))
+        fill_scale_rows(nc.sync, wb_s_raw, wb_scales)
         nc.sync.dma_start(page_list[:], offs)
-        load_scale_rows(nc.sync, pages_s, pages_scales)
+        fill_scale_rows(nc.sync, pages_s, pages_scales, range(2, 4))
         nc.sync.dma_start(out=wa_w_raw[:].bitcast(I32), in_=wa_words[0].bitcast(I32))
         load_scale_rows(nc.sync, wa_s_raw, wa_scales)
         nc.sync.dma_start(column_list[:], offs3)
@@ -107,18 +114,14 @@ def tile_attend_matchtable_kernel(
         for half in range(2):
             cols = slice(half * HALF, (half + 1) * HALF)
             planes = tile([P, PACK, HALF], BF16, "h_planes%d" % half)
-            for pair in range(2):
-                acc = bank(2 * half + pair, [P, 2, HALF], "h_acc")
-                for e in range(2):
-                    t = 2 * pair + e
-                    nc.tensor.matmul_mx(
-                        out=acc[:, e, :],
-                        lhsT=wb_w[:, t * P:(t + 1) * P].bitcast(E4M3), lhsT_scale=wb_s[:, t * P:(t + 1) * P],
-                        rhs=note_w[:, cols].bitcast(E2M1), rhs_scale=note_s[:, cols], start=True, stop=True)
-                for e in range(2):
-                    t = 2 * pair + e
-                    nc.scalar.activation(
-                        out=planes[:, t, :], in_=acc[:, e, :], func=ACT.Copy, scale=kf_cols[:, t:t + 1])
+            for t in range(PACK):
+                acc = bank(PACK * half + t, [P, HALF], "h_acc")
+                nc.tensor.matmul_mx(
+                    out=acc[:],
+                    lhsT=wb_w[:, t * P:(t + 1) * P].bitcast(E4M3), lhsT_scale=wb_s[:, t * P:(t + 1) * P],
+                    rhs=note_w[:, cols].bitcast(E2M1), rhs_scale=note_s[:, cols], start=True, stop=True)
+                nc.scalar.activation(
+                    out=planes[:, t, :], in_=acc[:], func=ACT.Copy, scale=kf_cols[:, t:t + 1])
             h_planes.append(planes)
 
         page_w = tile([P, I], U32, "page_w")
@@ -126,13 +129,13 @@ def tile_attend_matchtable_kernel(
         page_s = tile([P, I], U8, "page_s")
         nc.vector.tensor_copy(page_s[:], pages_s[:].indirect(page_list[:]))
         wa_w = tile([P, K], U16, "wa_w")
-        wa_s = tile([P, K], U8, "wa_s")
+        wa_s = tile([P, K], U8, "wa_s", "staging2")
         deal(nc, wa_w[:], wa_w_raw[:], 8)
         deal(nc, wa_s[:].bitcast(I32), wa_s_raw[:].bitcast(I32), 2)
         z_grouped = []
         for chunk in range(4):
             cols = slice(chunk * P, (chunk + 1) * P)
-            acc = bank(4 + chunk, [P, PACK, P], "z_acc")
+            acc = bank(chunk, [P, PACK, P], "z_acc")
             for t in range(PACK):
                 nc.tensor.matmul_mx(
                     out=acc[:, t, :],
@@ -145,34 +148,31 @@ def tile_attend_matchtable_kernel(
 
         h_codes = tile([P, J], U32, "h_codes")
         h_scales = tile([P, J], U8, "h_scales")
-        h_grouped = []
+        h_grouped = tile([P, J * PACK], BF16, "h_grouped", "staging0")
         for half in range(2):
-            grouped = tile([P, HALF, PACK], BF16, "h_grouped%d" % half)
             nc.vector.tensor_copy(
-                out=grouped[:].rearrange("p (c i) t -> p c t i", i=4),
+                out=h_grouped[:, half * HALF * PACK:(half + 1) * HALF * PACK].rearrange(
+                    "p (c i t) -> p c t i", i=4, t=PACK),
                 in_=h_planes[half][:].rearrange("p t (c i) -> p c t i", i=4))
-            h_grouped.append(grouped)
         for half in range(2):
             cols = slice(half * HALF, (half + 1) * HALF)
             nc.vector.quantize_mx(
                 out=h_codes[:, cols].bitcast(E4M3), scales=h_scales[:, cols],
-                in_=h_grouped[half][:].rearrange("p j t -> p (j t)"))
+                in_=h_grouped[:, half * HALF * PACK:(half + 1) * HALF * PACK])
 
-        z_codes = []
-        for chunk in range(4):
-            codes = tile([P, P], U32, "z_codes%d" % chunk)
-            scales = tile([P, P], U8, "z_scales%d" % chunk)
+        def quantise_z(chunk):
+            codes = tile([P, P], U32, "z_codes%d" % chunk, "z_codes%d" % (chunk % 2))
+            scales = tile([P, P], U8, "z_scales%d" % chunk, "z_scales%d" % (chunk % 2))
             nc.vector.quantize_mx(
                 out=codes[:].bitcast(E4M3), scales=scales[:],
                 in_=z_grouped[chunk][:].rearrange("p i t -> p (i t)"))
-            z_codes.append((codes, scales))
-
-        for chunk in range(4):
-            codes, scales = z_codes[chunk]
-            acc = bank(chunk, [P, J], "s_acc")
+            acc = bank(4 + chunk, [P, J], "s_acc")
             nc.tensor.matmul_mx(
                 out=acc[:], lhsT=codes[:].bitcast(E4M3), lhsT_scale=scales[:],
                 rhs=h_codes[:].bitcast(E4M3), rhs_scale=h_scales[:], start=True, stop=True)
+            return acc
+
+        def finish(chunk, acc):
             table = tile([P, J], F32, "table%d" % chunk)
             top = tile([P, 1], F32, "top%d" % chunk)
             nc.vector.tensor_scalar(
@@ -185,3 +185,10 @@ def tile_attend_matchtable_kernel(
             nc.scalar.activation(
                 out=result[:], in_=table[:].indirect(column_list[:]), func=ACT.Exp, bias=minus_top[:])
             nc.sync.dma_start(out=out[chunk * P:(chunk + 1) * P, :], in_=result[:])
+
+        ahead = quantise_z(0)
+        for chunk in range(4):
+            acc = ahead
+            if chunk < 3:
+                ahead = quantise_z(chunk + 1)
+            finish(chunk, acc)

@@ -74,6 +74,8 @@ def tile_attend_matchtable_kernel(
         kf_rows = tile([P, P], F32, "kf_rows")
         identity = tile([P, P], F32, "identity")
 
+        nc.gpsimd.memset(notes_s[:].bitcast(I32), 0)
+        nc.vector.memset(wb_s_raw[:].bitcast(I32), 0)
         nc.vector.memset(pages_s[0:64, :].bitcast(I32), 0)
         nc.vector.memset(wa_s_raw[:].bitcast(I32), 0)
         nc.gpsimd.memset(kf_rows[:], 0.0)
@@ -84,12 +86,12 @@ def tile_attend_matchtable_kernel(
 
         nc.sync.dma_start(out=notes_w[:].bitcast(I32), in_=notes_words[0].bitcast(I32))
         nc.sync.dma_start(note_list[:], offs2)
-        fill_scale_rows(nc.sync, notes_s, notes_scales)
+        load_scale_rows(nc.sync, notes_s, notes_scales)
         nc.sync.dma_start(
             out=wb_w_raw[:].bitcast(I32), in_=wb_words[0].rearrange("p n t -> p (n t)").bitcast(I32))
         nc.sync.dma_start(
             out=pages_w[:].bitcast(I32), in_=pages_words[0].rearrange("p n t -> p (n t)").bitcast(I32))
-        fill_scale_rows(nc.sync, wb_s_raw, wb_scales)
+        load_scale_rows(nc.sync, wb_s_raw, wb_scales)
         nc.sync.dma_start(page_list[:], offs)
         fill_scale_rows(nc.sync, pages_s, pages_scales, range(2, 4))
         nc.sync.dma_start(out=wa_w_raw[:].bitcast(I32), in_=wa_words[0].bitcast(I32))

from contextlib import ExitStack

import concourse.mybir as mybir
from concourse.masks import make_identity

F32 = mybir.dt.float32
BF16 = mybir.dt.bfloat16
I32 = mybir.dt.int32
U32 = mybir.dt.uint32
U16 = mybir.dt.uint16
U8 = mybir.dt.uint8
E4M3 = mybir.dt.float8_e4m3fn_x4
E2M1 = mybir.dt.float4_e2m1fn_x4
ACT = mybir.ActivationFunctionType
ALU = mybir.AluOpType

P = 128
PACK = 4
D, K, T, U, I, J, C = 512, 512, 2048, 1024, 512, 512, 256
HALF = 256
FLOPS = 2 * (D * K * I + D * K * J + K * I * J)


def load_scale_rows(queue, plane, rows, quadrants=range(4)):
    for quadrant in quadrants:
        queue.dma_start(
            out=plane[32 * quadrant:32 * quadrant + 4, :].bitcast(I32),
            in_=rows[0, 4 * quadrant:4 * quadrant + 4, :].bitcast(I32))


def fill_scale_rows(queue, plane, rows, quadrants=range(4)):
    for quadrant in quadrants:
        four = rows[0, 4 * quadrant:4 * quadrant + 4, :].bitcast(I32)
        queue.dma_start(
            out=plane[32 * quadrant:32 * quadrant + 32, :].bitcast(I32),
            in_=four.unsqueeze(0).broadcast_to([8, 4, four.shape[1]]))


def deal(nc, dst, src, run):
    nc.vector.tensor_copy(
        out=dst.rearrange("p (t q r) -> p t q r", t=PACK, r=run),
        in_=src.rearrange("p (q t r) -> p t q r", t=PACK, r=run),
    )


def tile_attend_matchtable_kernel(
    tc, pages_words, pages_scales, wa_words, wa_scales, notes_words, notes_scales,
    wb_words, wb_scales, kf, offs, offs2, offs3, out,
):
    nc = tc.nc
    with ExitStack() as ctx:
        lists = ctx.enter_context(tc.tile_pool(name="lists", bufs=1))
        sb = ctx.enter_context(tc.tile_pool(name="sb", bufs=1))
        psum = ctx.enter_context(tc.psum_pool(name="psum", bufs=1))

        def tile(shape, dtype, name, tag=None):
            return sb.tile(shape, dtype, name=name, tag=tag or name, align_bytes=64)

        def bank(n, shape, name):
            return psum.tile(shape, F32, name=name, tag="bank%d" % n)

        page_list = lists.tile([P, I // 16], U16, name="page_list")
        note_list = lists.tile([P, J // 16], U16, name="note_list")
        column_list = lists.tile([P, C // 16], U16, name="column_list")

        pages_w = tile([P, T], U32, "pages_w")
        pages_s = tile([P, T], U8, "pages_s", "staging2")
        notes_w = tile([P, U], U16, "notes_w")
        notes_s = tile([P, U], U8, "notes_s")
        wa_w_raw = tile([P, K], U16, "wa_w_raw")
        wa_s_raw = tile([P, K], U8, "wa_s_raw", "staging0")
        wb_w_raw = tile([P, K], U32, "wb_w_raw")
        wb_s_raw = tile([P, K], U8, "wb_s_raw")
        kf_rows = tile([P, P], F32, "kf_rows")
        identity = tile([P, P], F32, "identity")

        nc.gpsimd.memset(notes_s[:].bitcast(I32), 0)
        nc.vector.memset(wb_s_raw[:].bitcast(I32), 0)
        nc.vector.memset(pages_s[0:64, :].bitcast(I32), 0)
        nc.vector.memset(wa_s_raw[:].bitcast(I32), 0)
        nc.gpsimd.memset(kf_rows[:], 0.0)
        nc.gpsimd.dma_start(
            out=kf_rows[0:PACK, :], in_=kf.rearrange("(q t r) o -> t q (r o)", t=PACK, r=8))
        make_identity(nc, identity[:])
        load_scale_rows(nc.gpsimd, pages_s, pages_scales, range(0, 2))

        nc.sync.dma_start(out=notes_w[:].bitcast(I32), in_=notes_words[0].bitcast(I32))
        nc.sync.dma_start(note_list[:], offs2)
        load_scale_rows(nc.sync, notes_s, notes_scales)
        nc.sync.dma_start(
            out=wb_w_raw[:].bitcast(I32), in_=wb_words[0].rearrange("p n t -> p (n t)").bitcast(I32))
        nc.sync.dma_start(
            out=pages_w[:].bitcast(I32), in_=pages_words[0].rearrange("p n t -> p (n t)").bitcast(I32))
        load_scale_rows(nc.sync, wb_s_raw, wb_scales)
        nc.sync.dma_start(page_list[:], offs)
        fill_scale_rows(nc.sync, pages_s, pages_scales, range(2, 4))
        nc.sync.dma_start(out=wa_w_raw[:].bitcast(I32), in_=wa_words[0].bitcast(I32))
        load_scale_rows(nc.sync, wa_s_raw, wa_scales)
        nc.sync.dma_start(column_list[:], offs3)

        kf_turned = bank(7, [P, P], "kf_turned")
        nc.tensor.transpose(kf_turned[:], kf_rows[:], identity[:])
        kf_cols = tile([P, PACK], F32, "kf_cols")
        nc.scalar.copy(out=kf_cols[:], in_=kf_turned[:, 0:PACK])

        note_w = tile([P, J], U16, "note_w")
        note_s = tile([P, J], U8, "note_s")
        nc.vector.tensor_copy(note_w[:], notes_w[:].indirect(note_list[:]))
        nc.vector.tensor_copy(note_s[:], notes_s[:].indirect(note_list[:]))

        wb_w = tile([P, K], U32, "wb_w")
        wb_s = tile([P, K], U8, "wb_s")
        deal(nc, wb_w[:], wb_w_raw[:], 8)
        deal(nc, wb_s[:].bitcast(I32), wb_s_raw[:].bitcast(I32), 2)
        h_planes = []
        for half in range(2):
            cols = slice(half * HALF, (half + 1) * HALF)
            planes = tile([P, PACK, HALF], BF16, "h_planes%d" % half)
            for t in range(PACK):
                acc = bank(PACK * half + t, [P, HALF], "h_acc")
                nc.tensor.matmul_mx(
                    out=acc[:],
                    lhsT=wb_w[:, t * P:(t + 1) * P].bitcast(E4M3), lhsT_scale=wb_s[:, t * P:(t + 1) * P],
                    rhs=note_w[:, cols].bitcast(E2M1), rhs_scale=note_s[:, cols], start=True, stop=True)
                nc.scalar.activation(
                    out=planes[:, t, :], in_=acc[:], func=ACT.Copy, scale=kf_cols[:, t:t + 1])
            h_planes.append(planes)

        page_w = tile([P, I], U32, "page_w")
        nc.vector.tensor_copy(page_w[:], pages_w[:].indirect(page_list[:]))
        page_s = tile([P, I], U8, "page_s")
        nc.vector.tensor_copy(page_s[:], pages_s[:].indirect(page_list[:]))
        wa_w = tile([P, K], U16, "wa_w")
        wa_s = tile([P, K], U8, "wa_s", "staging2")
        deal(nc, wa_w[:], wa_w_raw[:], 8)
        deal(nc, wa_s[:].bitcast(I32), wa_s_raw[:].bitcast(I32), 2)
        z_grouped = []
        for chunk in range(4):
            cols = slice(chunk * P, (chunk + 1) * P)
            acc = bank(chunk, [P, PACK, P], "z_acc")
            for t in range(PACK):
                nc.tensor.matmul_mx(
                    out=acc[:, t, :],
                    lhsT=wa_w[:, t * P:(t + 1) * P].bitcast(E2M1), lhsT_scale=wa_s[:, t * P:(t + 1) * P],
                    rhs=page_w[:, cols].bitcast(E4M3), rhs_scale=page_s[:, cols],
                    start=True, stop=True)
            grouped = tile([P, P, PACK], BF16, "z_grouped%d" % chunk)
            nc.scalar.copy(out=grouped[:], in_=acc[:].rearrange("p t i -> p i t"))
            z_grouped.append(grouped)

        h_codes = tile([P, J], U32, "h_codes")
        h_scales = tile([P, J], U8, "h_scales")
        h_grouped = tile([P, J * PACK], BF16, "h_grouped", "staging0")
        for half in range(2):
            nc.vector.tensor_copy(
                out=h_grouped[:, half * HALF * PACK:(half + 1) * HALF * PACK].rearrange(
                    "p (c i t) -> p c t i", i=4, t=PACK),
                in_=h_planes[half][:].rearrange("p t (c i) -> p c t i", i=4))
        for half in range(2):
            cols = slice(half * HALF, (half + 1) * HALF)
            nc.vector.quantize_mx(
                out=h_codes[:, cols].bitcast(E4M3), scales=h_scales[:, cols],
                in_=h_grouped[:, half * HALF * PACK:(half + 1) * HALF * PACK])

        def quantise_z(chunk):
            codes = tile([P, P], U32, "z_codes%d" % chunk, "z_codes%d" % (chunk % 2))
            scales = tile([P, P], U8, "z_scales%d" % chunk, "z_scales%d" % (chunk % 2))
            nc.vector.quantize_mx(
                out=codes[:].bitcast(E4M3), scales=scales[:],
                in_=z_grouped[chunk][:].rearrange("p i t -> p (i t)"))
            acc = bank(4 + chunk, [P, J], "s_acc")
            nc.tensor.matmul_mx(
                out=acc[:], lhsT=codes[:].bitcast(E4M3), lhsT_scale=scales[:],
                rhs=h_codes[:].bitcast(E4M3), rhs_scale=h_scales[:], start=True, stop=True)
            return acc

        def finish(chunk, acc):
            table = tile([P, J], F32, "table%d" % chunk)
            top = tile([P, 1], F32, "top%d" % chunk)
            nc.vector.tensor_scalar(
                out=table[:], in0=acc[:], scalar1=1.0, scalar2=None, op0=ALU.mult, op1=ALU.max,
                accum_out=top[:])
            minus_top = tile([P, 1], F32, "minus_top%d" % chunk)
            nc.gpsimd.tensor_scalar(
                out=minus_top[:], in0=top[:], scalar1=-1.0, scalar2=0.0, op0=ALU.mult, op1=ALU.add)
            result = tile([P, C], F32, "result%d" % chunk)
            nc.scalar.activation(
                out=result[:], in_=table[:].indirect(column_list[:]), func=ACT.Exp, bias=minus_top[:])
            nc.sync.dma_start(out=out[chunk * P:(chunk + 1) * P, :], in_=result[:])

        ahead = quantise_z(0)
        for chunk in range(4):
            acc = ahead
            if chunk < 3:
                ahead = quantise_z(chunk + 1)
            finish(chunk, acc)
